import numpy as np, ml_dtypes
CORES = [40,41,42,43,44,45,46,47]
N = 8
import mx_ref
BF = ml_dtypes.bfloat16
def gentries(a):
    return np.ascontiguousarray(a.reshape(8, 16, -1).transpose(0, 2, 1)).reshape(8, -1)
def gtable(e):
    e = np.asarray(e); return np.ascontiguousarray(e.reshape(8, -1, 16).transpose(0, 2, 1)).reshape(128, -1).astype(np.int32)
def gcols(t, e):
    v = np.concatenate([t.reshape(8, 16, -1, 4), np.zeros((8, 16, 1, 4), BF)], axis=2)
    return np.ascontiguousarray(np.stack([v[g][:, e[g]] for g in range(8)])).reshape(128, -1)
def tile(rs):
    return np.stack(rs, axis=2).reshape(128, -1).astype(BF)
def pick(q, e):
    c = np.concatenate([q[0].reshape(128, -1, 4), np.zeros((128, 1, 4), np.uint8)], axis=1); s = np.concatenate([q[1], np.ones((16, 1), np.uint8)], axis=1)
    return (np.ascontiguousarray(c[:, e].reshape(128, -1)), np.ascontiguousarray(s[:, e]))
def join(*qs):
    return (np.concatenate([q[0] for q in qs], axis=1), np.concatenate([q[1] for q in qs], axis=1))
def put(q, e, v):
    c, s = q[0].reshape(128, -1, 4).copy(), q[1].copy(); c[:, e] = v[0].reshape(128, -1, 4); s[:, e] = v[1]
    return (c.reshape(128, -1), s)
def pk(c, s):
    return (np.ascontiguousarray(c), mx_ref.live(s))
def emit(q):
    return q[0], q[1]
def packed(v, rng):
    q = [mx_ref.quantize(np.ascontiguousarray(v[r])) for r in range(N)]
    return np.stack([a for a, b in q]), np.stack([mx_ref.plane(b, rng) for a, b in q])
def values_of_codes():
    e, c = np.zeros((128, 128, 4), np.float32), np.zeros((128, 2, 4), np.uint8)
    e[np.arange(128), np.arange(128), 0] = 1
    c[:127, :, 0] = np.arange(256).reshape(2, 128).T[:127]
    return mx_ref.matmul(mx_ref.quantize(e.reshape(128, 512).astype(BF)), (c.reshape(128, 8), np.full((16, 2), 127, np.uint8))).T.reshape(-1).astype(np.float64)
CODE_VALUE, SCALE_VALUE = values_of_codes(), 2.0 ** (np.arange(256) - 127.0)
def decode(q):
    return (CODE_VALUE[q[0]].reshape(16, 8, -1, 4) * SCALE_VALUE[q[1]][:, None, :, None] + 0.0).reshape(128, -1).astype(np.float32)
def f(rng, *shape):
    return mx_ref.flush((rng.standard_normal(shape, dtype=np.float32) * np.exp2(rng.integers(-2, 3, shape[:-1] + (1,)))).astype(BF))
def wide(rng, *shape, cols=0):
    v = rng.standard_normal(shape, dtype=np.float32) * np.exp2(rng.integers(-12, 13, shape)).astype(np.float32)
    if cols: v *= np.repeat(np.exp2(rng.integers(-cols, cols + 1, shape[:-2] + (1, shape[-1] // 4))) * (rng.random(shape[:-2] + (1, shape[-1] // 4)) > 0.0625), 4, axis=-1).astype(np.float32)
    return mx_ref.flush(v.astype(BF))
C, STAGES = 320, 6
STEP = [1, 2, 4]
def numbers_of(rng):
    return {"x": np.array(f(rng, N, 128, 4 * C)), "u": np.array(f(rng, N, 128, 512)), "v": np.array(f(rng, N, 128, 512))}
def stored(a, b, s):
    return {"ta": np.stack([gtable(a[r]) for r in range(N)]), "tb": np.stack([gtable(b[r]) for r in range(N)]), "st": np.stack([gtable(s[r]) for r in range(N)])}
def lists(rng):
    e = np.tile(np.arange(C), (N, 8, 1))
    return stored(rng.permuted(e, axis=2), rng.permuted(e, axis=2), rng.permuted(e, axis=2))
def layers(rng):
    return np.array(f(rng, N, 128, 2048)).reshape(N, 8, 16, 4, 8, 16, 4)
def weights(rng, w):
    c, p = packed(np.ascontiguousarray(w).reshape(N, 128, 2048), rng)
    return {"wc": c, "ws": p}
def setup_inputs(rng):
    return {**numbers_of(rng), **lists(rng), **weights(rng, layers(rng))}
def setup_inputs_ties(rng):
    d = numbers_of(rng)
    o = rng.permutation(N)
    k = rng.integers(-1, 2, (2, N, 8, C)).astype(np.float32)
    k[0, o[1]] = 1
    x = d["x"].reshape(N, 8, 16, C, 4)
    x[:, :, [0, 1, 8]] = 0
    x[:, :, 0, :, 0] = k[0].astype(BF)
    x[:, :, 1, :, 0] = k[1].astype(BF)
    c = np.ones(N, np.float32)
    c[o[0]] = 0
    c[o[2]] = -1
    u = d["u"].reshape(N, 128, 128, 4)
    u[:, :, ::16] = 0
    for h in range(0, 128, 16):
        u[:, h, h, 0] = c.astype(BF)
        u[:, h + 8, h, 0] = c.astype(BF)
    w = layers(rng)
    w[:, :, :, :, :, [0, 1, 8]] = 0
    for g in range(8): w[:, g, 1, 0, g, 8, 0] = 32.0
    return {"x": x.reshape(N, 128, 4 * C), "u": u.reshape(N, 128, 512), "v": d["v"], **lists(rng), **weights(rng, w)}
def setup_inputs_near(rng):
    d = numbers_of(rng)
    o = rng.permutation(N) % 2
    k = np.where(o == 0, 2.0 ** -30, 1.0).astype(np.float32)
    x = np.zeros((N, 8, 16, C, 4), np.float32)
    s = rng.integers(-1, 2, (N, 8, C)) * k[:, None, None]
    x[:, :, 0, :, 0] = 1.125 * s
    x[:, :, 1, :, 0] = -1.25 * s
    for r in range(N):
        for g in rng.permutation(8)[:4]: x[r, g, 0, rng.integers(C), 0] = 2.0 ** 30 * rng.choice([-1.0, 1.0])
    x[:, :, 10, :, 0] = rng.integers(-1, 2, (N, 8, C)) * 2.0 ** -30
    x[:, :, 11, :, 0] = 2.0 ** -30
    u = d["u"].reshape(N, 128, 128, 4)
    u[:, :, ::16] = 0
    for h in range(0, 128, 16):
        u[:, h, h, 0] = (1.125 * k).astype(BF)
        u[:, h + 1, h, 0] = k.astype(BF)
        u[:, h + 8, h, 0] = k.astype(BF)
    w = np.zeros((N, 8, 16, 4, 8, 16, 4), np.float32)
    for g in range(8):
        w[:, g, 10, 0, g, 8, 0] = 2.0 ** -7
        w[:, g, 11, 0, g, 9, 0] = 2.0 ** 7
    for r in range(N):
        for g in rng.permutation(8)[:4]:
            w[r, g, 10, 0, g, 8, 0] = 2.0 ** -11
            w[r, g, 10, 0, g, 13, 0] = -2.0 ** -11
            w[r, g, 12, 0, g, 8, 0] = 2.0 ** -8
            w[r, g, 12, 0, g, 13, 0] = 2.0 ** -8
            w[r, g, 11, 0, g, 9, 0] = 2.0 ** 5
            u[r, 16 * g + 8, 16 * g, 0] = 1.125 * float(k[r])
            u[r, 16 * g + 13, 16 * g, 0] = float(k[r])
    return {"x": x.reshape(N, 128, 4 * C).astype(BF), "u": u.reshape(N, 128, 512), "v": d["v"], **lists(rng), **weights(rng, w.astype(BF))}
def setup_inputs_odd(rng):
    d = numbers_of(rng)
    x = (1.0 + (2 * rng.integers(0, 64, (N, 8, 16, C, 4)) + 1) * 2.0 ** -7) * np.exp2(-rng.integers(0, 7, (N, 8, 16, C, 4)).astype(np.float64)) * rng.choice([-1.0, 1.0], (N, 8, 16, C, 4))
    x[:, :, 0, :, 0] = 1.96875 * 2.0 ** 8 * rng.choice([-1.0, 1.0], (N, 8, C))
    x[:, :, 1:3] = 0
    x[:, :, 1, :, 0] = (8 + rng.integers(0, 2, (N, 8, C))) * 2.0 ** -8
    x[:, :, 2, :, 0] = -2.0 ** -5
    a = np.exp2(rng.integers(-3, 4, (N, 8, C)).astype(np.float64))
    x[:, :, 8:] = 0
    x[:, :, 8, :, 0] = 1.125 * a
    x[:, :, 11, :, 0] = (8 + rng.integers(0, 2, (N, 8, C))) * 2.0 ** -7 * a
    x[:, :, 12, :, 0] = 2.0 ** -4 * a
    u = d["u"].reshape(N, 128, 128, 4)
    u[:, :, ::16] = 0
    for h in range(0, 128, 16):
        for i in (1, 2, 9, 10): u[:, h + i, h, 0] = 1.0
    w = layers(rng)
    w[:, :, :3] = 0
    w[:, :, :, :, :, :3] = 0
    w[:, :, :, :, :, 8:] = 0
    for g in range(8):
        w[:, g, 8, 0, g, 8, 0] = 28.0
        w[:, g, 11, 0, g, 9, 0] = 2.0 ** -5
        w[:, g, 12, 0, g, 10, 0] = -2.0 ** -5
    return {"x": x.astype(np.float32).reshape(N, 128, 4 * C).astype(BF), "u": u.reshape(N, 128, 512), "v": d["v"], **lists(rng), **weights(rng, w)}
def setup_inputs_ends(rng):
    d = numbers_of(rng)
    o, e, h = rng.permutation(N) % 4, rng.permutation(N) % 4, rng.permutation(N) % 2
    s = rng.choice([-1.0, 1.0], (N, 8, 8, C, 4))
    s[o == 0] = -1
    s[o == 1] = rng.choice([-1.0, 1.0], (N, 1, 1, C, 1))[o == 1]
    low = s * (0.9 + 0.1 * rng.random((N, 8, 8, C, 4))) * 2.0 ** 30
    low[o == 3] = s[o == 3] * 2.0 ** -30
    x = d["x"].astype(np.float32).reshape(N, 8, 16, C, 4)
    x[:, :, :8] = low
    size = np.where(o == 3, 2.0 ** -30, 2.0 ** 30)
    c = np.stack([rng.permutation(8) % 2 * 2.0 - 1.0 for r in range(N)]) * size[:, None]
    u = d["u"].reshape(N, 128, 128, 4)
    u[:, :, ::16] = c.astype(np.float32).astype(BF)[:, None, :, None]
    v = rng.choice([-1.0, 1.0], (N, 128, 512)) * size[:, None, None]
    a, b, t = [rng.integers(0, C, (N, 8, C)) for i in range(3)]
    a[e == 0], b[e == 0], t[e == 0] = C - 1, C - 1, C - 1
    a[e == 1], b[e == 1], t[e == 1] = 0, C - 1, 0
    a[e == 2], b[e == 2], t[e == 2] = C - 1 - np.arange(C), np.arange(C), (np.arange(C) + 1) % 2 * (C - 1)
    w = np.zeros((N, 128, 4, 128, 4), np.float32)
    i = np.flatnonzero(np.arange(128) % 16 >= 8)
    for k in range(4): w[:, i, k, i, k] = np.where(h == 0, 2.0 ** 8, 2.0 ** -8)[:, None] * rng.choice([-1.0, 1.0], (N, 64))
    return {"x": x.reshape(N, 128, 4 * C).astype(BF), "u": u.reshape(N, 128, 512), "v": v.astype(np.float32).astype(BF), **stored(a, b, t), **weights(rng, w.astype(BF))}
def setup_inputs_spread(rng):
    d = setup_inputs(rng)
    d["x"] = wide(rng, N, 128, 4 * C, cols=6)
    return d
def check_inputs(d):
    b = []
    for k in ("x", "u", "v"):
        a = np.abs(d[k].astype(np.float32))
        if not (np.isfinite(a).all() and ((a == 0) | (a >= 2.0 ** -30) & (a <= 2.0 ** 30)).all()): b.append("a value of " + k)
    for k in ("ta", "tb", "st"):
        if not ((d[k] >= 0) & (d[k] < C)).all(): b.append("an entry of " + k)
    none, least, most = [emit(mx_ref.quantize(np.full((128, 16), k, np.float32).astype(BF)))[1][0, 0] for k in (0.0, 2.0 ** -8, 2.0 ** 8)]
    for r in range(N):
        if ((d["wc"][r] == 0x7F) | (d["wc"][r] == 0xFF)).any(): b.append("wc: a code that is no number")
        s = mx_ref.live(d["ws"][r])
        if ((s != none) & ((s < least) | (s > most))).any(): b.append("ws: a scale out of range")
    return b
def at(t, s):
    return np.take_along_axis(t, s, axis=2)
def reference(x, u, v, ta, tb, st, wc, ws):
    qu = [mx_ref.quantize(u[r]) for r in range(N)]
    lay = [pk(wc[r], ws[r]) for r in range(N)]
    a, b, s = [np.stack([gentries(k[r]) for r in range(N)]).astype(np.int64) for k in (ta, tb, st)]
    now = [x[r] for r in range(N)]
    for step in STEP:
        q = [mx_ref.quantize(now[r]) for r in range(N)]
        bit = np.stack([mx_ref.matmul(qu[r], q[r])[::16] > 0 for r in range(N)])
        for k in range(STAGES):
            right = np.roll(at(bit, s), -1, axis=2)
            s = np.where(right, at(b, s), at(a, s))
        z = [gcols(decode(q[r]).astype(BF), s[r]) for r in range(N)]
        qz = [mx_ref.quantize(z[r]) for r in range(N)]
        made, change = [], []
        for r in range(N):
            p = r ^ step
            h = tile([mx_ref.matmul(pick(lay[r], np.arange(128 * k, 128 * k + 128)), qz[p]) * np.float32(0.03125) for k in range(4)])
            change.append(mx_ref.matmul(qu[r], mx_ref.quantize(h))[::16] > 0)
            made.append((z[r].astype(np.float32) + gcols(h, s[p]).astype(np.float32)).astype(BF))
        c = np.stack(change)
        a, b = np.where(c, b, a), np.where(c, a, b)
        now = made
    y, op = np.zeros((N, 128, C), np.float32), np.zeros((N, 8, 3 * C), np.float32)
    oc, osc = np.zeros((N, 128, 4 * C), np.uint8), np.zeros((N, 16, C), np.uint8)
    for r in range(N):
        q = mx_ref.quantize(now[r])
        y[r] = mx_ref.matmul(mx_ref.quantize(v[r]), q)
        op[r] = np.concatenate([s[r], a[r], b[r]], axis=1)
        oc[r], osc[r] = emit(q)
    return {"y": y, "op": op, "oc": oc, "osc": osc}

@@ -1,0 +1,321 @@
+from concourse.mybir import dt, AluOpType, ActivationFunctionType
+
+STEP = [1, 2, 4]
+C, STAGES = 320, 6
+L = 2048
+BIG = 4096
+UP = 2.0 ** 60
+CUT = 12
+SCRATCH = {}
+
+
+def _declare(names, where, cols, dtype):
+    for n in names.split():
+        SCRATCH[n] = (where, [128, cols], dtype)
+
+
+F8, U8 = "float8_e4m3fn_x4", "uint8"
+_declare("sti tai tbi kp kk k20 e16 ee qq ic cc", "sbuf", 20, "int32")
+_declare("d32 dd", "sbuf", 32, "int32")
+_declare("lui", "sbuf", 8, "int32")
+_declare("lu", "sbuf", 8, "uint16")
+_declare("lk rho la lb ls lfa lfb sn0 sn1 sn2 pl0 pl1 pl2", "sbuf", 20, "uint16")
+_declare("lc o0 o1 sc", "sbuf", 22, "uint16")
+_declare("rr", "sbuf", 60, "float32")
+_declare("pp", "sbuf", 160, "float32")
+_declare("sm", "sbuf", 8, "float32")
+_declare("M G0 G1 E0 E1", "sbuf", 336, "float32")
+_declare("M0 idn b0 b4 b1 b2 b4s g1 g2 g3 x12 x320 fin tt pk NR EN yb", "sbuf", C, "float32")
+_declare("W W6", "sbuf", 3016, "float32")
+_declare("W4", "sbuf", 1280, "float32")
+_declare("ob", "sbuf", 960, "float32")
+_declare("one dg", "sbuf", 128, "bfloat16")
+_declare("ui vi", "sbuf", 512, "bfloat16")
+_declare("et", "sbuf", 2048, "bfloat16")
+_declare("xi ht z0 z1 z2 xn0 xn1 xn2", "sbuf", 4 * C, "bfloat16")
+_declare("t0 t1 t2 t3 h0 h1 h2 h3", "sbuf", C, "bfloat16")
+for _q, _p, _n in (("wq", "wp", 512), ("uq", "us", 128), ("urq", "urs", 128), ("vq", "vs", 128), ("eq", "es", 512), ("hq", "hp", C)):
+    _declare(_q, "sbuf", _n, F8)
+    _declare(_p, "sbuf", _n, U8)
+_declare("zq0 zq1 zq2 rq0 rq1 rq2 xq0 xq1 xq2 xq3", "sbuf", C, F8)
+_declare("zp0 zp1 zp2 rp0 rp1 rp2 xs0 xs1 xs2 xs3", "sbuf", C, U8)
+_declare("ps0 ps1 ps2 ps3 ps4 ps5 ps6", "psum", 512, "float32")
+SEMAPHORES = ("cv ct ca cg sent gotl0 gotl1 gotl2 gotz0 gotz1 gotz2 ld_st ld_x ld_ta ld_tb ld_u ld_wc ld_ws ld_v "
+              "sv_y sv_ops sv_opt sv_oc sv_os0 sv_os1 sv_os2 sv_os3").split()
+
+
+def rank_program(g, core, T, topo):
+    rank = T.rank_of(core)
+    if rank is None:
+        return
+    A, ACT = AluOpType, ActivationFunctionType
+    queues = {"v": g.vector, "t": g.tensor, "a": g.scalar, "g": g, "y": g.sync}
+    counter = {"v": "cv", "t": "ct", "a": "ca", "g": "cg"}
+    count = {}
+    known = {q: {} for q in queues}
+    told = {}
+    wrote, read = {}, {}
+
+    def learn(q, tokens):
+        need = {}
+        for s, n in tokens:
+            need[s] = max(need.get(s, 0), n)
+        for s in sorted(need):
+            n = need[s]
+            if known[q].get(s, 0) >= n:
+                continue
+            queues[q].wait_ge(T.sem[s], n)
+            known[q][s] = n
+            for k, m in told.get((s, n), {}).items():
+                known[q][k] = max(known[q].get(k, 0), m)
+
+    def op(q, call, rd, wr, sem=None, inc=1):
+        need = []
+        for k in rd:
+            need += wrote.get(k, [])
+        for k in wr:
+            need += wrote.get(k, []) + read.get(k, [])
+        learn(q, need)
+        s = sem or counter[q]
+        call().then_inc(T.sem[s], inc)
+        count[s] = count.get(s, 0) + inc
+        tok = (s, count[s])
+        told[tok] = dict(known[q])
+        for k in rd:
+            read.setdefault(k, []).append(tok)
+        for k in wr:
+            wrote[k], read[k] = [tok], []
+
+    V, S, P = g.vector, g.scalar, g.tensor
+
+    def load(q, name, out, in_, key):
+        op(q, lambda: queues[q].dma_start(out, in_), [], [key], sem="ld_" + name, inc=16)
+
+    def store(name, out, in_, rd):
+        op("y", lambda: g.sync.dma_start(out, in_), rd, [], sem="sv_" + name, inc=16)
+
+    def iota(out, pattern, base, cm, wr, f32=False):
+        if f32:
+            op("g", lambda: g.iota(out, pattern, base, cm, allow_small_or_imprecise_dtypes=True), [], [wr])
+        else:
+            op("g", lambda: g.iota(out, pattern, base, cm), [], [wr])
+
+    def ts(out, in0, s1, s2, o0, o1, rd, wr):
+        if o1 is None:
+            op("v", lambda: V.tensor_scalar(out, in0, s1, None, o0), rd, wr)
+        else:
+            op("v", lambda: V.tensor_scalar(out, in0, s1, s2, o0, o1), rd, wr)
+
+    def tt(out, a, b, o, rd, wr):
+        op("v", lambda: V.tensor_tensor(out, a, b, o), rd, wr)
+
+    def cpv(out, in_, rd, wr):
+        op("v", lambda: V.tensor_copy(out, in_), rd, wr)
+
+    def cpa(out, in_, rd, wr):
+        op("a", lambda: S.activation(out, in_, ACT.Copy), rd, wr)
+
+    def scan(out, d0, d1, init, o0, o1, rd, wr):
+        op("v", lambda: V.tensor_tensor_scan(out, d0, d1, init, o0, o1), rd, wr)
+
+    def plus(out, a, b, rd, wr):
+        scan(out, a, b, float(BIG), A.min, A.add, rd, wr)
+
+    def quant(codes, plane, tile, rd, wr):
+        op("v", lambda: V.quantize_mx(codes, plane, tile), rd, wr)
+
+    def mm(bank, lq, lp, rq, rp, rd):
+        op("t", lambda: P.matmul_mx(T["ps%d" % bank][:, 0:C], lq, lp, rq, rp, True, True), rd, ["ps%d" % bank])
+
+    load("y", "st", T.sti[:], T.st[:], "sti")
+    load("y", "x", T.xi[:], T.x[:], "xi")
+    load("a", "u", T.ui[:], T.u[:], "ui")
+    load("a", "ta", T.tai[:], T.ta[:], "tai")
+    load("y", "tb", T.tbi[:], T.tb[:], "tbi")
+    learn("y", wrote["xi"])
+    load("y", "wc", T.wq[:, :].bitcast(dt.uint8), T.wc[:, :], "wq")
+    load("y", "ws", T.wp[:, :], T.ws[:, :], "wp")
+    load("y", "v", T.vi[:], T.v[:], "vi")
+
+    op("v", lambda: V.memset(T.one[:], 1.0), [], ["one"])
+    iota(T.kp[:], [[0, 20]], 0, 1, "kp")
+    iota(T.d32[:], [[1, 2], [1, 16]], 127, -1, "d32")
+    iota(T.lui[:], [[16, 8]], 0, 0, "lui")
+    op("g", lambda: g.affine_select(T.dg[:], T.one[:], [[-1, 128]], A.is_equal, 0.0, 0, 1), ["one"], ["dg"])
+    iota(T.ic[:], [[-1, 20]], 19, 0, "ic")
+    iota(T.e16[:], [[16, 20]], 0, 0, "e16")
+    iota(T.idn[:], [[1, C]], 1, 0, "idn", True)
+    iota(T.b0[:], [[3, C]], 3 + BIG, 0, "b0", True)
+    for w in ("W", "W6"):
+        iota(T[w][:, 0:3], [[0, 3]], BIG + 3, 0, w + "x", True)
+        iota(T[w][:, 963:2051], [[0, 1088]], BIG + 3, 0, w + "y", True)
+    iota(T.b4[:], [[1, C]], BIG, 0, "b4", True)
+
+    op("v", lambda: V.memset(T.et[:], 0.0), [], ["etz"])
+    ts(T.kk[:], T.kp[:], 15, None, A.bitwise_and, None, ["kp"], ["kk"])
+    ts(T.dd[:], T.d32[:], 15, None, A.bitwise_and, None, ["d32"], ["dd"])
+    cpv(T.lk[:], T.kk[:], ["kk"], ["lk"])
+    cpv(T.lu[:], T.lui[:], ["lui"], ["lu"])
+    ts(T.pp[:, 0:32], T.dd[:], 0, 1.0 / UP / L, A.is_equal, A.mult, ["dd"], ["p0"])
+    ts(T.pp[:, 32:64], T.dd[:], 1, UP, A.is_equal, A.mult, ["dd"], ["p1"])
+    ts(T.pp[:, 64:96], T.dd[:], 2, None, A.is_ge, None, ["dd"], ["p2"])
+    ts(T.sm[:, 2:3], T.dd[:, 16:17], 2, UP, A.is_equal, A.mult, ["dd"], ["m1"])
+    ts(T.sm[:, 3:4], T.dd[:, 16:17], 1, None, A.is_ge, None, ["dd"], ["m2"])
+    ts(T.sm[:, 0:1], T.kk[:, 0:1], 15, None, A.is_equal, None, ["kk"], ["c1"])
+    ts(T.sm[:, 1:2], T.kk[:, 0:1], 15, 1.0 / UP, A.is_lt, A.mult, ["kk"], ["c2"])
+    ts(T.k20[:], T.kk[:], 20, None, A.mult, None, ["kk"], ["k20"])
+    tt(T.pp[:, 96:128], T.pp[:, 32:64], T.pp[:, 64:96], A.add, ["p1", "p2"], ["p12"])
+    tt(T.sm[:, 4:5], T.sm[:, 2:3], T.sm[:, 3:4], A.max, ["m1", "m2"], ["m3"])
+    tt(T.sm[:, 5:6], T.sm[:, 0:1], T.sm[:, 1:2], A.add, ["c1", "c2"], ["cp"])
+    tt(T.pp[:, 128:160], T.pp[:, 96:128], T.pp[:, 0:32], A.add, ["p12", "p0"], ["pm"])
+    tt(T.cc[:], T.k20[:], T.ic[:], A.add, ["k20", "ic"], ["cc"])
+    tt(T.ee[:], T.e16[:], T.kk[:], A.add, ["e16", "kk"], ["ee"])
+    cpv(T.M[:, 0:16], T.pp[:, 128:144], ["pm"], ["Ma"])
+    cpv(T.lc[:, 1:21], T.cc[:], ["cc"], ["lc1"])
+    cpv(T.lc[:, 0:1], T.k20[:, 0:1], ["k20"], ["lc0"])
+    ts(T.qq[:], T.ee[:], -9.5, 0.05, A.add, A.mult, ["ee"], ["qq"])
+    ts(T.rr[:, 0:20], T.ee[:], -16.0, 304.0, A.mult, A.add, ["ee"], ["r1"])
+    ts(T.rr[:, 20:40], T.qq[:], 321.0, None, A.mult, None, ["qq"], ["r2"])
+    tt(T.rr[:, 40:60], T.rr[:, 0:20], T.rr[:, 20:40], A.add, ["r1", "r2"], ["r3"])
+    cpv(T.rho[:], T.rr[:, 40:60], ["r3"], ["rho"])
+    CP = T.sm[:, 5:6]
+    for b in range(4):
+        cpa(T.et[:, 512 * b + b:512 * b + 512:4], T.dg[:], ["dg", "etz"], ["et%d" % b])
+    cpa(T.M[:, 16:336], T.pp[:, 144:160].indirect(T.lk[:]), ["pm", "lk"], ["Mb"])
+    cpa(T.M0[:], T.pp[:, 112:128].indirect(T.lk[:]), ["p12", "lk"], ["M0"])
+    quant(T.eq[:], T.es[:], T.et[:], ["et0", "et1", "et2", "et3", "etz"], ["eq"])
+    tt(T.M[:, 16:17], T.sm[:, 4:5], T.pp[:, 16:17], A.max, ["m3", "p0"], ["Mb"])
+
+    quant(T.uq[:], T.us[:], T.ui[:], ["ui"], ["uq"])
+    cpv(T.urq[:, 0:128].bitcast(dt.uint32), T.uq[:, 0:128].bitcast(dt.uint32).indirect(T.lu[:, 0:8]), ["uq", "lu"], ["urq"])
+    cpa(T.urs[:, 0:128], T.us[:, 0:128].indirect(T.lu[:, 0:8]), ["uq", "lu"], ["urs"])
+    cpv(T.ls[:], T.sti[:], ["sti"], ["ls"])
+    cpv(T.la[:], T.tai[:], ["tai"], ["la"])
+    cpv(T.lb[:], T.tbi[:], ["tbi"], ["lb"])
+
+    def scores(r):
+        mm(4, T.urq[:], T.urs[:], T["xq%d" % r][:], T["xs%d" % r][:], ["urq", "urs", "xq%d" % r])
+
+    def unpack(r):
+        for b in range(4):
+            mm(b, T.eq[:, 128 * b:128 * b + 128], T.es[:, 128 * b:128 * b + 128], T["xq%d" % r][:], T["xs%d" % r][:], ["eq", "xq%d" % r])
+
+    def pick(G, E, o, less):
+        scan(T[E][:, :], T.M[:, :], T[G][:, :], 0.0, A.mult, A.add, [G + "a", G + "b", "Ma", "Mb"], [E])
+        ts(T[o][:, 1:21], T[E][:, 31:336:16], CP, -float(less), A.mult, A.add, [E, "cp"], [o + "m"])
+        ts(T[o][:, 0:1], T[E][:, 335:336], CP, -float(less), A.mult, A.add, [E, "cp"], [o + "d"])
+
+    cpv(T.NR[:], T.idn[:].indirect(T.ls[:]), ["idn", "ls"], ["NRa", "NRb"])
+    quant(T.xq0[:], T.xs0[:], T.xi[:], ["xi"], ["xq0"])
+    scores(0)
+    unpack(0)
+    cpv(T.G1[:, :], T.NR[:].indirect(T.lc[:, 0:21]), ["NRa", "NRb", "lc0", "lc1"], ["G1a", "G1b"])
+    pick("G1", "E1", "sc", 1)
+    cpa(T.W6[:, 3:961:3], T.idn[:].indirect(T.la[:]), ["idn", "la"], ["W60"])
+    cpa(T.W6[:, 4:962:3], T.idn[:].indirect(T.lb[:]), ["idn", "lb"], ["W61"])
+    cpa(T.W6[:, 5:963:3], T.W6[:, 3:961:3], ["W60"], ["W62"])
+    W6K = ["W60", "W61", "W62", "W6x", "W6y", "W63", "W64", "W65"]
+    WK = ["W0", "W1", "W2", "Wd", "We", "Wx", "Wy"]
+    less = BIG + BIG // L
+
+    base = "b0"
+    for r in range(3):
+        other = T.cores[rank ^ STEP[r]]
+        rid, pid = topo.addr(other)[0:2]
+        mask, ne = topo.mask(core, other), len(topo.engines(core, other))
+        z, zq, zp, rq, rp, sn, pl, xn = [n + str(r) for n in ("z", "zq", "zp", "rq", "rp", "sn", "pl", "xn")]
+        if r == 0:
+            ts(T.tt[:], T.ps4[:, 0:C], 0.0, float(L), A.is_gt, A.mult, ["ps4"], ["tt"])
+        plus(T.pk[:], T.tt[:], T[base][:], ["tt", base], ["pk"])
+        cpa(T.W[:, 3:961:3], T.pk[:].indirect(T.la[:]), ["pk", "la"], ["W0"])
+        cpv(T.W[:, 4:962:3], T.pk[:].indirect(T.lb[:]), ["pk", "lb"], ["W1"])
+        cpv(T.G0[:, :], T.pk[:].indirect(T.sc[:, 0:21]), ["pk", "scm", "scd"], ["G0a", "G0b"])
+        cpa(T.W[:, 5:963:3], T.W[:, 3:961:3], ["W0"], ["W2"])
+        pick("G0", "E0", "o0", less)
+        cpa(T.W[:, 2051:2691], T.W[:, 3:643], ["W0", "W1", "W2"], ["Wd"])
+        cpv(T.W[:, 2691:3011], T.W[:, 643:963], ["W0", "W1", "W2"], ["We"])
+        gaps = [(T["t%d" % b][:], T["ps%d" % b][:, 0:C], ["ps%d" % b], ["t%d" % b]) for b in range(4)]
+        if r == 0:
+            for i in range(3):
+                gaps.insert(2 * i + 1, (T.W6[:, 2051 + 320 * i:2371 + 320 * i], T.W6[:, 3 + 320 * i:323 + 320 * i], W6K[0:3], [W6K[5 + i]]))
+        for n in range(1, STAGES + 1):
+            o, G, E, on = "o%d" % ((n + 1) % 2), "G%d" % (n % 2), "E%d" % (n % 2), "o%d" % (n % 2)
+            win, wk = (T.W, WK) if n < STAGES else (T.W6, W6K)
+            cpv(T[G][:, 0:16 * CUT], win[:, 0:3011].indirect(T[o][:, 0:CUT]), wk + [o + "m", o + "d"], [G + "a"])
+            cpa(T[G][:, 16 * CUT:336], win[:, 0:3011].indirect(T[o][:, CUT:21]), wk + [o + "m", o + "d"], [G + "b"])
+            if n < STAGES:
+                for i in range(2 if r == 0 else 1):
+                    if gaps:
+                        cpa(*gaps.pop(0))
+                pick(G, E, on, less)
+        cpv(T.NR[:, 0:160], T.G0[:, 16:336].indirect(T.rho[:, 0:10]), ["G0a", "G0b", "rho"], ["NRa"])
+        cpa(T.NR[:, 160:320], T.G0[:, 16:336].indirect(T.rho[:, 10:20]), ["G0a", "G0b", "rho"], ["NRb"])
+        scan(T.EN[:], T.M0[:], T.NR[:], 0.0, A.mult, A.add, ["NRa", "NRb", "M0"], ["EN"])
+        ts(T[sn][:], T.EN[:, 15:320:16], CP, -1.0, A.mult, A.add, ["EN", "cp"], [sn])
+        for b in range(4):
+            (cpv if b < 2 else cpa)(T[z][:, b:4 * C:4], T["t%d" % b][:].indirect(T[sn][:]), ["t%d" % b, sn], [z + str(b)])
+        learn("g", wrote[sn])
+        g.remote_dma(T[pl][:, :], T[sn][:, :], T.sem["gotl%d" % r], T.sem.sent, pid, rid, mask)
+        quant(T[zq][:], T[zp][:], T[z][:], [z + str(b) for b in range(4)], [zq])
+        learn("g", wrote[zq])
+        g.remote_dma(T[rq][:, :].bitcast(dt.uint8), T[zq][:, :].bitcast(dt.uint8), T.sem["gotz%d" % r], T.sem.sent, pid, rid, mask)
+        g.remote_dma(T[rp][:, :], T[zp][:, :], T.sem["gotz%d" % r], T.sem.sent, pid, rid, mask)
+        count["sent"] = count.get("sent", 0) + 3 * ne
+        wrote[pl], wrote[rq] = [("gotl%d" % r, ne)], [("gotz%d" % r, 2 * ne)]
+        if r < 2:
+            pick("G0", "E1", "sc", 1)
+        if r == 0:
+            quant(T.vq[:], T.vs[:], T.vi[:], ["vi"], ["vq"])
+        if r == 1:
+            cpa(T.W4[:, 0:320], T.W6[:, 3:961:3], ["W60"], ["W4a"])
+            cpa(T.W4[:, 320:640], T.W6[:, 4:962:3], ["W61"], ["W4b"])
+            cpa(T.W4[:, 640:1280], T.W4[:, 0:640], ["W4a", "W4b"], ["W4c"])
+        if r == 2:
+            ts(T.x320[:], T.x12[:], 320.0, None, A.mult, None, ["x12"], ["x320"])
+            plus(T.b4s[:], T.x320[:], T.b4[:], ["x320", "b4"], ["b4s"])
+            op("a", lambda: S.activation(T.ob[:, 0:320], T.NR[:], ACT.Identity, bias=-1.0), ["NRa", "NRb"], ["obs"])
+            store("ops", T.op[:, 0:320], T.ob[0:128:16, 0:320], ["obs"])
+        for b in range(4):
+            mm(b, T.wq[:, 128 * b:128 * b + 128], T.wp[:, 128 * b:128 * b + 128], T[rq][:], T[rp][:], ["wq", "wp", rq])
+        for b in range(4):
+            hb, pb = T["h%d" % b], T["ps%d" % b]
+            op("a", lambda: S.activation(hb[:], pb[:, 0:C], ACT.Copy, scale=0.03125), ["ps%d" % b], ["h%d" % b])
+            tt(T[xn][:, b:4 * C:4], hb[:].indirect(T[pl][:]), T[z][:, b:4 * C:4], A.add, ["h%d" % b, pl, z + str(b)], [xn + str(b)])
+        for b in range(4):
+            cpa(T.ht[:, b:4 * C:4], T["h%d" % b][:], ["h%d" % b], ["ht%d" % b])
+        xq, xs = "xq%d" % (r + 1), "xs%d" % (r + 1)
+        quant(T[xq][:], T[xs][:], T[xn][:], [xn + str(b) for b in range(4)], [xq])
+        if r < 2:
+            scores(r + 1)
+        else:
+            store("oc", T.oc[:, :], T.xq3[:, :].bitcast(dt.uint8), [xq])
+            for k in range(4):
+                store("os%d" % k, T.osc[4 * k:4 * k + 4, :], T.xs3[32 * k:32 * k + 4, :], [xq])
+            mm(6, T.vq[:], T.vs[:], T.xq3[:], T.xs3[:], ["vq", xq])
+            cpa(T.yb[:], T.ps6[:, 0:C], ["ps6"], ["yb"])
+            store("y", T.y[:, :], T.yb[:], ["yb"])
+        quant(T.hq[:], T.hp[:], T.ht[:], ["ht%d" % b for b in range(4)], ["hq"])
+        mm(5, T.urq[:], T.urs[:], T.hq[:], T.hp[:], ["urq", "urs", "hq"])
+        if r < 2:
+            unpack(r + 1)
+            ts(T.tt[:], T.ps4[:, 0:C], 0.0, float(L), A.is_gt, A.mult, ["ps4"], ["tt"])
+        if r == 0:
+            ts(T.g1[:], T.ps5[:, 0:C], 0.0, None, A.is_gt, None, ["ps5"], ["g1"])
+            plus(T.b1[:], T.g1[:], T.b0[:], ["g1", "b0"], ["b1"])
+            base = "b1"
+        elif r == 1:
+            ts(T.g2[:], T.ps5[:, 0:C], 0.0, None, A.is_gt, None, ["ps5"], ["g2"])
+            tt(T.x12[:], T.g1[:], T.g2[:], A.not_equal, ["g1", "g2"], ["x12"])
+            plus(T.b2[:], T.x12[:], T.b0[:], ["x12", "b0"], ["b2"])
+            base = "b2"
+        else:
+            ts(T.g3[:], T.ps5[:, 0:C], 0.0, 320.0, A.is_gt, A.mult, ["ps5"], ["g3"])
+            plus(T.fin[:], T.g3[:], T.b4s[:], ["g3", "b4s"], ["fin"])
+            scan(T.EN[:], T.M0[:], T.fin[:], 0.0, A.mult, A.add, ["fin", "M0"], ["EN"])
+            ts(T.lfa[:], T.EN[:, 15:320:16], CP, -float(BIG), A.mult, A.add, ["EN", "cp"], ["lfa"])
+            ts(T.lfb[:], T.EN[:, 15:320:16], CP, 320.0 - BIG, A.mult, A.add, ["EN", "cp"], ["lfb"])
+            w4 = ["W4a", "W4b", "W4c"]
+            op("a", lambda: S.activation(T.ob[:, 320:640], T.W4[:, :].indirect(T.lfa[:]), ACT.Identity, bias=-1.0), w4 + ["lfa"], ["oba"])
+            ts(T.ob[:, 640:960], T.W4[:, :].indirect(T.lfb[:]), -1.0, None, A.add, None, w4 + ["lfb"], ["obb"])
+            store("opt", T.op[:, 320:960], T.ob[0:128:16, 320:960], ["oba", "obb"])
+    learn("g", [(s, n) for s, n in count.items()])

@@ -5,7 +5,7 @@ C, STAGES = 320, 6
 L = 2048
 BIG = 4096
 UP = 2.0 ** 60
-CUT = 12
+CUT = 10
 SCRATCH = {}
 
 
@@ -25,20 +25,20 @@ _declare("rr", "sbuf", 60, "float32")
 _declare("pp", "sbuf", 160, "float32")
 _declare("sm", "sbuf", 8, "float32")
 _declare("M G0 G1 E0 E1", "sbuf", 336, "float32")
-_declare("M0 idn b0 b4 b1 b2 b4s g1 g2 g3 x12 x320 fin tt pk NR EN yb", "sbuf", C, "float32")
+_declare("M0 idn b0 b4 uu b4s g1 g2 g3 x12 x320 fin tt pk NR EN yb", "sbuf", C, "float32")
 _declare("W W6", "sbuf", 3016, "float32")
 _declare("W4", "sbuf", 1280, "float32")
 _declare("ob", "sbuf", 960, "float32")
 _declare("one dg", "sbuf", 128, "bfloat16")
 _declare("ui vi", "sbuf", 512, "bfloat16")
 _declare("et", "sbuf", 2048, "bfloat16")
-_declare("xi ht z0 z1 z2 xn0 xn1 xn2", "sbuf", 4 * C, "bfloat16")
-_declare("t0 t1 t2 t3 h0 h1 h2 h3", "sbuf", C, "bfloat16")
-for _q, _p, _n in (("wq", "wp", 512), ("uq", "us", 128), ("urq", "urs", 128), ("vq", "vs", 128), ("eq", "es", 512), ("hq", "hp", C)):
+_declare("xi ht z za xn0 xn1 xn2", "sbuf", 4 * C, "bfloat16")
+_declare("t0 t1 t2 t3 w0 w1 w2 w3 h0 h1 h2 h3", "sbuf", C, "bfloat16")
+for _q, _p, _n in (("wq", "wp", 512), ("uq", "us", 128), ("urq", "urs", 128), ("vq", "vs", 128), ("eq", "es", 512), ("hq", "hp", C), ("zq", "zp", C)):
     _declare(_q, "sbuf", _n, F8)
     _declare(_p, "sbuf", _n, U8)
-_declare("zq0 zq1 zq2 rq0 rq1 rq2 xq0 xq1 xq2 xq3", "sbuf", C, F8)
-_declare("zp0 zp1 zp2 rp0 rp1 rp2 xs0 xs1 xs2 xs3", "sbuf", C, U8)
+_declare("rq0 rq1 rq2 xq0 xq1 xq2 xq3", "sbuf", C, F8)
+_declare("rp0 rp1 rp2 xs0 xs1 xs2 xs3", "sbuf", C, U8)
 _declare("ps0 ps1 ps2 ps3 ps4 ps5 ps6", "psum", 512, "float32")
 SEMAPHORES = ("cv ct ca cg sent gotl0 gotl1 gotl2 gotz0 gotz1 gotz2 ld_st ld_x ld_ta ld_tb ld_u ld_wc ld_ws ld_v "
               "sv_y sv_ops sv_opt sv_oc sv_os0 sv_os1 sv_os2 sv_os3").split()
@@ -100,6 +100,9 @@ def rank_program(g, core, T, topo):
         else:
             op("g", lambda: g.iota(out, pattern, base, cm), [], [wr])
 
+    def cpg(out, in_, rd, wr):
+        op("g", lambda: g.affine_select(out, in_, [[1, C]], A.is_ge, 0.0, 0, 0), rd, wr)
+
     def ts(out, in0, s1, s2, o0, o1, rd, wr):
         if o1 is None:
             op("v", lambda: V.tensor_scalar(out, in0, s1, None, o0), rd, wr)
@@ -146,12 +149,14 @@ def rank_program(g, core, T, topo):
     iota(T.e16[:], [[16, 20]], 0, 0, "e16")
     iota(T.idn[:], [[1, C]], 1, 0, "idn", True)
     iota(T.b0[:], [[3, C]], 3 + BIG, 0, "b0", True)
-    for w in ("W", "W6"):
+
+    def unnamed(w):
         iota(T[w][:, 0:3], [[0, 3]], BIG + 3, 0, w + "x", True)
         iota(T[w][:, 963:2051], [[0, 1088]], BIG + 3, 0, w + "y", True)
-    iota(T.b4[:], [[1, C]], BIG, 0, "b4", True)
 
-    op("v", lambda: V.memset(T.et[:], 0.0), [], ["etz"])
+    unnamed("W")
+    op("v", lambda: V.memset(T.et[:, 0:1024], 0.0), [], ["etz"])
+    cpa(T.et[:, 1024:2048], T.et[:, 0:1024], ["etz"], ["ety"])
     ts(T.kk[:], T.kp[:], 15, None, A.bitwise_and, None, ["kp"], ["kk"])
     ts(T.dd[:], T.d32[:], 15, None, A.bitwise_and, None, ["d32"], ["dd"])
     cpv(T.lk[:], T.kk[:], ["kk"], ["lk"])
@@ -180,142 +185,166 @@ def rank_program(g, core, T, topo):
     cpv(T.rho[:], T.rr[:, 40:60], ["r3"], ["rho"])
     CP = T.sm[:, 5:6]
     for b in range(4):
-        cpa(T.et[:, 512 * b + b:512 * b + 512:4], T.dg[:], ["dg", "etz"], ["et%d" % b])
+        cpa(T.et[:, 512 * b + b:512 * b + 512:4], T.dg[:], ["dg", "etz", "ety"], ["et%d" % b])
     cpa(T.M[:, 16:336], T.pp[:, 144:160].indirect(T.lk[:]), ["pm", "lk"], ["Mb"])
-    cpa(T.M0[:], T.pp[:, 112:128].indirect(T.lk[:]), ["p12", "lk"], ["M0"])
-    quant(T.eq[:], T.es[:], T.et[:], ["et0", "et1", "et2", "et3", "etz"], ["eq"])
+    cpv(T.ls[:], T.sti[:], ["sti"], ["ls"])
+    cpa(T.NR[:], T.idn[:].indirect(T.ls[:]), ["idn", "ls"], ["NRa", "NRb"])
+    cpa(T.G1[:, :], T.NR[:].indirect(T.lc[:, 0:21]), ["NRa", "NRb", "lc0", "lc1"], ["G1a", "G1b"])
+    quant(T.eq[:], T.es[:], T.et[:], ["et0", "et1", "et2", "et3", "etz", "ety"], ["eq"])
     tt(T.M[:, 16:17], T.sm[:, 4:5], T.pp[:, 16:17], A.max, ["m3", "p0"], ["Mb"])
 
     quant(T.uq[:], T.us[:], T.ui[:], ["ui"], ["uq"])
     cpv(T.urq[:, 0:128].bitcast(dt.uint32), T.uq[:, 0:128].bitcast(dt.uint32).indirect(T.lu[:, 0:8]), ["uq", "lu"], ["urq"])
     cpa(T.urs[:, 0:128], T.us[:, 0:128].indirect(T.lu[:, 0:8]), ["uq", "lu"], ["urs"])
-    cpv(T.ls[:], T.sti[:], ["sti"], ["ls"])
     cpv(T.la[:], T.tai[:], ["tai"], ["la"])
     cpv(T.lb[:], T.tbi[:], ["tbi"], ["lb"])
 
     def scores(r):
         mm(4, T.urq[:], T.urs[:], T["xq%d" % r][:], T["xs%d" % r][:], ["urq", "urs", "xq%d" % r])
 
-    def unpack(r):
-        for b in range(4):
-            mm(b, T.eq[:, 128 * b:128 * b + 128], T.es[:, 128 * b:128 * b + 128], T["xq%d" % r][:], T["xs%d" % r][:], ["eq", "xq%d" % r])
+    def unpack(b, q, p):
+        mm(b, T.eq[:, 128 * b:128 * b + 128], T.es[:, 128 * b:128 * b + 128], T[q][:], T[p][:], ["eq", q])
 
-    def pick(G, E, o, less):
+    def row(G, E):
         scan(T[E][:, :], T.M[:, :], T[G][:, :], 0.0, A.mult, A.add, [G + "a", G + "b", "Ma", "Mb"], [E])
+
+    def offsets(E, o, less):
         ts(T[o][:, 1:21], T[E][:, 31:336:16], CP, -float(less), A.mult, A.add, [E, "cp"], [o + "m"])
         ts(T[o][:, 0:1], T[E][:, 335:336], CP, -float(less), A.mult, A.add, [E, "cp"], [o + "d"])
 
-    cpv(T.NR[:], T.idn[:].indirect(T.ls[:]), ["idn", "ls"], ["NRa", "NRb"])
+    def partner(r):
+        other = T.cores[rank ^ STEP[r]]
+        return topo.addr(other)[0:2] + (topo.mask(core, other), len(topo.engines(core, other)))
+
+    def send_state(r):
+        rid, pid, mask, ne = partner(r)
+        xq, xs, rq, rp, sem = [n + str(r) for n in ("xq", "xs", "rq", "rp", "gotz")]
+        learn("g", wrote[xq])
+        g.remote_dma(T[rq][:, :].bitcast(dt.uint8), T[xq][:, :].bitcast(dt.uint8), T.sem[sem], T.sem.sent, pid, rid, mask)
+        g.remote_dma(T[rp][:, :], T[xs][:, :], T.sem[sem], T.sem.sent, pid, rid, mask)
+        count["sent"] = count.get("sent", 0) + 2 * ne
+        wrote[rq] = [(sem, 2 * ne)]
+
     quant(T.xq0[:], T.xs0[:], T.xi[:], ["xi"], ["xq0"])
     scores(0)
-    unpack(0)
-    cpv(T.G1[:, :], T.NR[:].indirect(T.lc[:, 0:21]), ["NRa", "NRb", "lc0", "lc1"], ["G1a", "G1b"])
-    pick("G1", "E1", "sc", 1)
+    for b in range(4):
+        unpack(b, "xq0", "xs0")
+    row("G1", "E1")
+    offsets("E1", "sc", 1)
+    send_state(0)
     cpa(T.W6[:, 3:961:3], T.idn[:].indirect(T.la[:]), ["idn", "la"], ["W60"])
     cpa(T.W6[:, 4:962:3], T.idn[:].indirect(T.lb[:]), ["idn", "lb"], ["W61"])
-    cpa(T.W6[:, 5:963:3], T.W6[:, 3:961:3], ["W60"], ["W62"])
     W6K = ["W60", "W61", "W62", "W6x", "W6y", "W63", "W64", "W65"]
-    WK = ["W0", "W1", "W2", "Wd", "We", "Wx", "Wy"]
+    WK = ["W0", "W1", "W2", "W3", "W4a1", "W4b1", "W5", "Wx", "Wy"]
     less = BIG + BIG // L
+    ts(T.tt[:], T.ps4[:, 0:C], 0.0, float(L), A.is_gt, A.mult, ["ps4"], ["tt"])
+    plus(T.pk[:], T.tt[:], T.b0[:], ["tt", "b0"], ["pk"])
 
-    base = "b0"
     for r in range(3):
-        other = T.cores[rank ^ STEP[r]]
-        rid, pid = topo.addr(other)[0:2]
-        mask, ne = topo.mask(core, other), len(topo.engines(core, other))
-        z, zq, zp, rq, rp, sn, pl, xn = [n + str(r) for n in ("z", "zq", "zp", "rq", "rp", "sn", "pl", "xn")]
-        if r == 0:
-            ts(T.tt[:], T.ps4[:, 0:C], 0.0, float(L), A.is_gt, A.mult, ["ps4"], ["tt"])
-        plus(T.pk[:], T.tt[:], T[base][:], ["tt", base], ["pk"])
+        rid, pid, mask, ne = partner(r)
+        rq, rp, sn, pl, xn = [n + str(r) for n in ("rq", "rp", "sn", "pl", "xn")]
         cpa(T.W[:, 3:961:3], T.pk[:].indirect(T.la[:]), ["pk", "la"], ["W0"])
-        cpv(T.W[:, 4:962:3], T.pk[:].indirect(T.lb[:]), ["pk", "lb"], ["W1"])
         cpv(T.G0[:, :], T.pk[:].indirect(T.sc[:, 0:21]), ["pk", "scm", "scd"], ["G0a", "G0b"])
+        cpv(T.W[:, 4:962:3], T.pk[:].indirect(T.lb[:]), ["pk", "lb"], ["W1"])
         cpa(T.W[:, 5:963:3], T.W[:, 3:961:3], ["W0"], ["W2"])
-        pick("G0", "E0", "o0", less)
-        cpa(T.W[:, 2051:2691], T.W[:, 3:643], ["W0", "W1", "W2"], ["Wd"])
-        cpv(T.W[:, 2691:3011], T.W[:, 643:963], ["W0", "W1", "W2"], ["We"])
-        gaps = [(T["t%d" % b][:], T["ps%d" % b][:, 0:C], ["ps%d" % b], ["t%d" % b]) for b in range(4)]
+        cpg(T.W[:, 2051:3009:3], T.W[:, 3:961:3], ["W0"], ["W3"])
+        cpa(T.W[:, 2053:3011:3], T.W[:, 3:961:3], ["W0"], ["W5"])
+        row("G0", "E0")
+        cpv(T.W[:, 2052:2530:3], T.W[:, 4:482:3], ["W1"], ["W4a1"])
+        cpa(T.W[:, 2532:3010:3], T.W[:, 484:962:3], ["W1"], ["W4b1"])
+        offsets("E0", "o0", less)
         if r == 0:
-            for i in range(3):
-                gaps.insert(2 * i + 1, (T.W6[:, 2051 + 320 * i:2371 + 320 * i], T.W6[:, 3 + 320 * i:323 + 320 * i], W6K[0:3], [W6K[5 + i]]))
+            unnamed("W6")
+            cpg(T.W6[:, 5:963:3], T.W6[:, 3:961:3], ["W60"], ["W62"])
+            cpg(T.W6[:, 2051:3009:3], T.W6[:, 3:961:3], ["W60"], ["W63"])
+            cpg(T.W6[:, 2052:3010:3], T.W6[:, 4:962:3], ["W61"], ["W64"])
+            cpg(T.W6[:, 2053:3011:3], T.W6[:, 3:961:3], ["W60"], ["W65"])
+            iota(T.b4[:], [[1, C]], BIG, 0, "b4", True)
+        gaps = [(T["t%d" % b][:], T["ps%d" % b][:, 0:C], ["ps%d" % b], ["t%d" % b], b) for b in range(4)]
+        gaps += [(T["w%d" % b][:], T["ps%d" % b][:, 0:C], ["ps%d" % b], ["w%d" % b], None) for b in range(2)]
         for n in range(1, STAGES + 1):
             o, G, E, on = "o%d" % ((n + 1) % 2), "G%d" % (n % 2), "E%d" % (n % 2), "o%d" % (n % 2)
             win, wk = (T.W, WK) if n < STAGES else (T.W6, W6K)
             cpv(T[G][:, 0:16 * CUT], win[:, 0:3011].indirect(T[o][:, 0:CUT]), wk + [o + "m", o + "d"], [G + "a"])
-            cpa(T[G][:, 16 * CUT:336], win[:, 0:3011].indirect(T[o][:, CUT:21]), wk + [o + "m", o + "d"], [G + "b"])
+            cpa(T[G][:, 16 * CUT:336], win[:, 0:3011].indirect(T[o][:, CUT:21]), wk + [o + "m"], [G + "b"])
             if n < STAGES:
-                for i in range(2 if r == 0 else 1):
-                    if gaps:
-                        cpa(*gaps.pop(0))
-                pick(G, E, on, less)
+                for out, in_, rd, wr, b in [gaps.pop(0) for i in range(2 if n == 1 else 1)]:
+                    cpa(out, in_, rd, wr)
+                    if b is not None:
+                        unpack(b, rq, rp)
+                row(G, E)
+                offsets(E, on, less)
         cpv(T.NR[:, 0:160], T.G0[:, 16:336].indirect(T.rho[:, 0:10]), ["G0a", "G0b", "rho"], ["NRa"])
         cpa(T.NR[:, 160:320], T.G0[:, 16:336].indirect(T.rho[:, 10:20]), ["G0a", "G0b", "rho"], ["NRb"])
-        scan(T.EN[:], T.M0[:], T.NR[:], 0.0, A.mult, A.add, ["NRa", "NRb", "M0"], ["EN"])
+        if r == 0:
+            cpa(T.M0[:], T.pp[:, 112:128].indirect(T.lk[:]), ["p12", "lk"], ["M0"])
+        scan(T.EN[:], T.M[:, 16:336], T.NR[:], 0.0, A.mult, A.add, ["NRa", "NRb", "Mb"], ["EN"])
         ts(T[sn][:], T.EN[:, 15:320:16], CP, -1.0, A.mult, A.add, ["EN", "cp"], [sn])
-        for b in range(4):
-            (cpv if b < 2 else cpa)(T[z][:, b:4 * C:4], T["t%d" % b][:].indirect(T[sn][:]), ["t%d" % b, sn], [z + str(b)])
         learn("g", wrote[sn])
         g.remote_dma(T[pl][:, :], T[sn][:, :], T.sem["gotl%d" % r], T.sem.sent, pid, rid, mask)
-        quant(T[zq][:], T[zp][:], T[z][:], [z + str(b) for b in range(4)], [zq])
-        learn("g", wrote[zq])
-        g.remote_dma(T[rq][:, :].bitcast(dt.uint8), T[zq][:, :].bitcast(dt.uint8), T.sem["gotz%d" % r], T.sem.sent, pid, rid, mask)
-        g.remote_dma(T[rp][:, :], T[zp][:, :], T.sem["gotz%d" % r], T.sem.sent, pid, rid, mask)
-        count["sent"] = count.get("sent", 0) + 3 * ne
-        wrote[pl], wrote[rq] = [("gotl%d" % r, ne)], [("gotz%d" % r, 2 * ne)]
+        count["sent"] += ne
+        wrote[pl] = [("gotl%d" % r, ne)]
+        for b in range(4):
+            (cpv if b < 2 else cpa)(T.z[:, b:4 * C:4], T["t%d" % b][:].indirect(T[sn][:]), ["t%d" % b, sn], ["z%d" % b])
+        for b in range(2, 4):
+            (cpv if b == 2 else cpa)(T["w%d" % b][:], T["ps%d" % b][:, 0:C], ["ps%d" % b], ["w%d" % b])
+        for b in range(4):
+            (cpv if b < 2 else cpa)(T.za[:, b:4 * C:4], T["w%d" % b][:].indirect(T[pl][:]), ["w%d" % b, pl], ["za%d" % b])
+        quant(T.zq[:], T.zp[:], T.za[:], ["za%d" % b for b in range(4)], ["zq"])
+        for b in range(4):
+            mm(b, T.wq[:, 128 * b:128 * b + 128], T.wp[:, 128 * b:128 * b + 128], T.zq[:], T.zp[:], ["wq", "wp", "zq"])
         if r < 2:
-            pick("G0", "E1", "sc", 1)
+            row("G0", "E1")
+            offsets("E1", "sc", 1)
         if r == 0:
             quant(T.vq[:], T.vs[:], T.vi[:], ["vi"], ["vq"])
-        if r == 1:
-            cpa(T.W4[:, 0:320], T.W6[:, 3:961:3], ["W60"], ["W4a"])
-            cpa(T.W4[:, 320:640], T.W6[:, 4:962:3], ["W61"], ["W4b"])
-            cpa(T.W4[:, 640:1280], T.W4[:, 0:640], ["W4a", "W4b"], ["W4c"])
         if r == 2:
             ts(T.x320[:], T.x12[:], 320.0, None, A.mult, None, ["x12"], ["x320"])
             plus(T.b4s[:], T.x320[:], T.b4[:], ["x320", "b4"], ["b4s"])
             op("a", lambda: S.activation(T.ob[:, 0:320], T.NR[:], ACT.Identity, bias=-1.0), ["NRa", "NRb"], ["obs"])
             store("ops", T.op[:, 0:320], T.ob[0:128:16, 0:320], ["obs"])
         for b in range(4):
-            mm(b, T.wq[:, 128 * b:128 * b + 128], T.wp[:, 128 * b:128 * b + 128], T[rq][:], T[rp][:], ["wq", "wp", rq])
-        for b in range(4):
             hb, pb = T["h%d" % b], T["ps%d" % b]
             op("a", lambda: S.activation(hb[:], pb[:, 0:C], ACT.Copy, scale=0.03125), ["ps%d" % b], ["h%d" % b])
-            tt(T[xn][:, b:4 * C:4], hb[:].indirect(T[pl][:]), T[z][:, b:4 * C:4], A.add, ["h%d" % b, pl, z + str(b)], [xn + str(b)])
+            tt(T[xn][:, b:4 * C:4], hb[:].indirect(T[pl][:]), T.z[:, b:4 * C:4], A.add, ["h%d" % b, pl, "z%d" % b], [xn + str(b)])
         for b in range(4):
             cpa(T.ht[:, b:4 * C:4], T["h%d" % b][:], ["h%d" % b], ["ht%d" % b])
+        if r == 1:
+            for i, key in enumerate(("W4a", "W4b", "W4c", "W4d")):
+                cpg(T.W4[:, 320 * i:320 * i + 320], T.W6[:, 3 + i % 2:961 + i % 2:3], ["W6%d" % (i % 2)], [key])
         xq, xs = "xq%d" % (r + 1), "xs%d" % (r + 1)
-        quant(T[xq][:], T[xs][:], T[xn][:], [xn + str(b) for b in range(4)], [xq])
         if r < 2:
+            quant(T[xq][:], T[xs][:], T[xn][:], [xn + str(b) for b in range(4)], [xq])
             scores(r + 1)
-        else:
-            store("oc", T.oc[:, :], T.xq3[:, :].bitcast(dt.uint8), [xq])
-            for k in range(4):
-                store("os%d" % k, T.osc[4 * k:4 * k + 4, :], T.xs3[32 * k:32 * k + 4, :], [xq])
-            mm(6, T.vq[:], T.vs[:], T.xq3[:], T.xs3[:], ["vq", xq])
-            cpa(T.yb[:], T.ps6[:, 0:C], ["ps6"], ["yb"])
-            store("y", T.y[:, :], T.yb[:], ["yb"])
-        quant(T.hq[:], T.hp[:], T.ht[:], ["ht%d" % b for b in range(4)], ["hq"])
-        mm(5, T.urq[:], T.urs[:], T.hq[:], T.hp[:], ["urq", "urs", "hq"])
-        if r < 2:
-            unpack(r + 1)
+            send_state(r + 1)
+            quant(T.hq[:], T.hp[:], T.ht[:], ["ht%d" % b for b in range(4)], ["hq"])
+            mm(5, T.urq[:], T.urs[:], T.hq[:], T.hp[:], ["urq", "urs", "hq"])
+            for b in range(4):
+                unpack(b, xq, xs)
+            gk = "g%d" % (r + 1)
             ts(T.tt[:], T.ps4[:, 0:C], 0.0, float(L), A.is_gt, A.mult, ["ps4"], ["tt"])
-        if r == 0:
-            ts(T.g1[:], T.ps5[:, 0:C], 0.0, None, A.is_gt, None, ["ps5"], ["g1"])
-            plus(T.b1[:], T.g1[:], T.b0[:], ["g1", "b0"], ["b1"])
-            base = "b1"
-        elif r == 1:
-            ts(T.g2[:], T.ps5[:, 0:C], 0.0, None, A.is_gt, None, ["ps5"], ["g2"])
-            tt(T.x12[:], T.g1[:], T.g2[:], A.not_equal, ["g1", "g2"], ["x12"])
-            plus(T.b2[:], T.x12[:], T.b0[:], ["x12", "b0"], ["b2"])
-            base = "b2"
-        else:
-            ts(T.g3[:], T.ps5[:, 0:C], 0.0, 320.0, A.is_gt, A.mult, ["ps5"], ["g3"])
-            plus(T.fin[:], T.g3[:], T.b4s[:], ["g3", "b4s"], ["fin"])
-            scan(T.EN[:], T.M0[:], T.fin[:], 0.0, A.mult, A.add, ["fin", "M0"], ["EN"])
-            ts(T.lfa[:], T.EN[:, 15:320:16], CP, -float(BIG), A.mult, A.add, ["EN", "cp"], ["lfa"])
-            ts(T.lfb[:], T.EN[:, 15:320:16], CP, 320.0 - BIG, A.mult, A.add, ["EN", "cp"], ["lfb"])
-            w4 = ["W4a", "W4b", "W4c"]
-            op("a", lambda: S.activation(T.ob[:, 320:640], T.W4[:, :].indirect(T.lfa[:]), ACT.Identity, bias=-1.0), w4 + ["lfa"], ["oba"])
-            ts(T.ob[:, 640:960], T.W4[:, :].indirect(T.lfb[:]), -1.0, None, A.add, None, w4 + ["lfb"], ["obb"])
-            store("opt", T.op[:, 320:960], T.ob[0:128:16, 320:960], ["oba", "obb"])
+            ts(T[gk][:], T.ps5[:, 0:C], 0.0, None, A.is_gt, None, ["ps5"], [gk])
+            plus(T.uu[:], T.tt[:], T.b0[:], ["tt", "b0"], ["uu"])
+            if r == 1:
+                tt(T.x12[:], T.g1[:], T.g2[:], A.not_equal, ["g1", "g2"], ["x12"])
+                gk = "x12"
+            plus(T.pk[:], T[gk][:], T.uu[:], [gk, "uu"], ["pk"])
+    quant(T.hq[:], T.hp[:], T.ht[:], ["ht%d" % b for b in range(4)], ["hq"])
+    mm(5, T.urq[:], T.urs[:], T.hq[:], T.hp[:], ["urq", "urs", "hq"])
+    quant(T.xq3[:], T.xs3[:], T.xn2[:], ["xn2%d" % b for b in range(4)], ["xq3"])
+    mm(6, T.vq[:], T.vs[:], T.xq3[:], T.xs3[:], ["vq", "xq3"])
+    store("oc", T.oc[:, :], T.xq3[:, :].bitcast(dt.uint8), ["xq3"])
+    for k in range(4):
+        store("os%d" % k, T.osc[4 * k:4 * k + 4, :], T.xs3[32 * k:32 * k + 4, :], ["xq3"])
+    cpa(T.yb[:], T.ps6[:, 0:C], ["ps6"], ["yb"])
+    store("y", T.y[:, :], T.yb[:], ["yb"])
+    ts(T.g3[:], T.ps5[:, 0:C], 0.0, 320.0, A.is_gt, A.mult, ["ps5"], ["g3"])
+    plus(T.fin[:], T.g3[:], T.b4s[:], ["g3", "b4s"], ["fin"])
+    scan(T.EN[:], T.M0[:], T.fin[:], 0.0, A.mult, A.add, ["fin", "M0"], ["EN"])
+    ts(T.lfa[:], T.EN[:, 15:320:16], CP, -float(BIG), A.mult, A.add, ["EN", "cp"], ["lfa"])
+    ts(T.lfb[:], T.EN[:, 15:320:16], CP, 320.0 - BIG, A.mult, A.add, ["EN", "cp"], ["lfb"])
+    w4 = ["W4a", "W4b", "W4c", "W4d"]
+    op("a", lambda: S.activation(T.ob[:, 320:640], T.W4[:, :].indirect(T.lfa[:]), ACT.Identity, bias=-1.0), w4 + ["lfa"], ["oba"])
+    ts(T.ob[:, 640:960], T.W4[:, :].indirect(T.lfb[:]), -1.0, None, A.add, None, w4 + ["lfb"], ["obb"])
+    store("opt", T.op[:, 320:960], T.ob[0:128:16, 320:960], ["oba", "obb"])
     learn("g", [(s, n) for s, n in count.items()])

from concourse.mybir import dt, AluOpType, ActivationFunctionType

STEP = [1, 2, 4]
C, STAGES = 320, 6
L = 2048
BIG = 4096
UP = 2.0 ** 60
CUT = 10
SCRATCH = {}


def _declare(names, where, cols, dtype):
    for n in names.split():
        SCRATCH[n] = (where, [128, cols], dtype)


F8, U8 = "float8_e4m3fn_x4", "uint8"
_declare("sti tai tbi kp kk k20 e16 ee qq ic cc", "sbuf", 20, "int32")
_declare("d32 dd", "sbuf", 32, "int32")
_declare("lui", "sbuf", 8, "int32")
_declare("lu", "sbuf", 8, "uint16")
_declare("lk rho la lb ls lfa lfb sn0 sn1 sn2 pl0 pl1 pl2", "sbuf", 20, "uint16")
_declare("lc o0 o1 sc", "sbuf", 22, "uint16")
_declare("rr", "sbuf", 60, "float32")
_declare("pp", "sbuf", 160, "float32")
_declare("sm", "sbuf", 8, "float32")
_declare("M G0 G1 E0 E1", "sbuf", 336, "float32")
_declare("M0 idn b0 b4 uu b4s g1 g2 g3 x12 x320 fin tt pk NR EN yb", "sbuf", C, "float32")
_declare("W W6", "sbuf", 3016, "float32")
_declare("W4", "sbuf", 1280, "float32")
_declare("ob", "sbuf", 960, "float32")
_declare("one dg", "sbuf", 128, "bfloat16")
_declare("ui vi", "sbuf", 512, "bfloat16")
_declare("et", "sbuf", 2048, "bfloat16")
_declare("xi ht z za xn0 xn1 xn2", "sbuf", 4 * C, "bfloat16")
_declare("t0 t1 t2 t3 w0 w1 w2 w3 h0 h1 h2 h3", "sbuf", C, "bfloat16")
for _q, _p, _n in (("wq", "wp", 512), ("uq", "us", 128), ("urq", "urs", 128), ("vq", "vs", 128), ("eq", "es", 512), ("hq", "hp", C), ("zq", "zp", C)):
    _declare(_q, "sbuf", _n, F8)
    _declare(_p, "sbuf", _n, U8)
_declare("rq0 rq1 rq2 xq0 xq1 xq2 xq3", "sbuf", C, F8)
_declare("rp0 rp1 rp2 xs0 xs1 xs2 xs3", "sbuf", C, U8)
_declare("ps0 ps1 ps2 ps3 ps4 ps5 ps6", "psum", 512, "float32")
SEMAPHORES = ("cv ct ca cg sent gotl0 gotl1 gotl2 gotz0 gotz1 gotz2 ld_st ld_x ld_ta ld_tb ld_u ld_wc ld_ws ld_v "
              "sv_y sv_ops sv_opt sv_oc sv_os0 sv_os1 sv_os2 sv_os3").split()


def rank_program(g, core, T, topo):
    rank = T.rank_of(core)
    if rank is None:
        return
    A, ACT = AluOpType, ActivationFunctionType
    queues = {"v": g.vector, "t": g.tensor, "a": g.scalar, "g": g, "y": g.sync}
    counter = {"v": "cv", "t": "ct", "a": "ca", "g": "cg"}
    count = {}
    known = {q: {} for q in queues}
    told = {}
    wrote, read = {}, {}

    def learn(q, tokens):
        need = {}
        for s, n in tokens:
            need[s] = max(need.get(s, 0), n)
        for s in sorted(need):
            n = need[s]
            if known[q].get(s, 0) >= n:
                continue
            queues[q].wait_ge(T.sem[s], n)
            known[q][s] = n
            for k, m in told.get((s, n), {}).items():
                known[q][k] = max(known[q].get(k, 0), m)

    def op(q, call, rd, wr, sem=None, inc=1):
        need = []
        for k in rd:
            need += wrote.get(k, [])
        for k in wr:
            need += wrote.get(k, []) + read.get(k, [])
        learn(q, need)
        s = sem or counter[q]
        call().then_inc(T.sem[s], inc)
        count[s] = count.get(s, 0) + inc
        tok = (s, count[s])
        told[tok] = dict(known[q])
        for k in rd:
            read.setdefault(k, []).append(tok)
        for k in wr:
            wrote[k], read[k] = [tok], []

    V, S, P = g.vector, g.scalar, g.tensor

    def load(q, name, out, in_, key):
        op(q, lambda: queues[q].dma_start(out, in_), [], [key], sem="ld_" + name, inc=16)

    def store(name, out, in_, rd):
        op("y", lambda: g.sync.dma_start(out, in_), rd, [], sem="sv_" + name, inc=16)

    def iota(out, pattern, base, cm, wr, f32=False):
        if f32:
            op("g", lambda: g.iota(out, pattern, base, cm, allow_small_or_imprecise_dtypes=True), [], [wr])
        else:
            op("g", lambda: g.iota(out, pattern, base, cm), [], [wr])

    def cpg(out, in_, rd, wr):
        op("g", lambda: g.affine_select(out, in_, [[1, C]], A.is_ge, 0.0, 0, 0), rd, wr)

    def ts(out, in0, s1, s2, o0, o1, rd, wr):
        if o1 is None:
            op("v", lambda: V.tensor_scalar(out, in0, s1, None, o0), rd, wr)
        else:
            op("v", lambda: V.tensor_scalar(out, in0, s1, s2, o0, o1), rd, wr)

    def tt(out, a, b, o, rd, wr):
        op("v", lambda: V.tensor_tensor(out, a, b, o), rd, wr)

    def cpv(out, in_, rd, wr):
        op("v", lambda: V.tensor_copy(out, in_), rd, wr)

    def cpa(out, in_, rd, wr):
        op("a", lambda: S.activation(out, in_, ACT.Copy), rd, wr)

    def scan(out, d0, d1, init, o0, o1, rd, wr):
        op("v", lambda: V.tensor_tensor_scan(out, d0, d1, init, o0, o1), rd, wr)

    def plus(out, a, b, rd, wr):
        scan(out, a, b, float(BIG), A.min, A.add, rd, wr)

    def quant(codes, plane, tile, rd, wr):
        op("v", lambda: V.quantize_mx(codes, plane, tile), rd, wr)

    def mm(bank, lq, lp, rq, rp, rd):
        op("t", lambda: P.matmul_mx(T["ps%d" % bank][:, 0:C], lq, lp, rq, rp, True, True), rd, ["ps%d" % bank])

    load("y", "st", T.sti[:], T.st[:], "sti")
    load("y", "x", T.xi[:], T.x[:], "xi")
    load("a", "u", T.ui[:], T.u[:], "ui")
    load("a", "ta", T.tai[:], T.ta[:], "tai")
    load("y", "tb", T.tbi[:], T.tb[:], "tbi")
    learn("y", wrote["xi"])
    load("y", "wc", T.wq[:, :].bitcast(dt.uint8), T.wc[:, :], "wq")
    load("y", "ws", T.wp[:, :], T.ws[:, :], "wp")
    load("y", "v", T.vi[:], T.v[:], "vi")

    op("v", lambda: V.memset(T.one[:], 1.0), [], ["one"])
    iota(T.kp[:], [[0, 20]], 0, 1, "kp")
    iota(T.d32[:], [[1, 2], [1, 16]], 127, -1, "d32")
    iota(T.lui[:], [[16, 8]], 0, 0, "lui")
    op("g", lambda: g.affine_select(T.dg[:], T.one[:], [[-1, 128]], A.is_equal, 0.0, 0, 1), ["one"], ["dg"])
    iota(T.ic[:], [[-1, 20]], 19, 0, "ic")
    iota(T.e16[:], [[16, 20]], 0, 0, "e16")
    iota(T.idn[:], [[1, C]], 1, 0, "idn", True)
    iota(T.b0[:], [[3, C]], 3 + BIG, 0, "b0", True)

    def unnamed(w):
        iota(T[w][:, 0:3], [[0, 3]], BIG + 3, 0, w + "x", True)
        iota(T[w][:, 963:2051], [[0, 1088]], BIG + 3, 0, w + "y", True)

    unnamed("W")
    op("v", lambda: V.memset(T.et[:, 0:1024], 0.0), [], ["etz"])
    cpa(T.et[:, 1024:2048], T.et[:, 0:1024], ["etz"], ["ety"])
    ts(T.kk[:], T.kp[:], 15, None, A.bitwise_and, None, ["kp"], ["kk"])
    ts(T.dd[:], T.d32[:], 15, None, A.bitwise_and, None, ["d32"], ["dd"])
    cpv(T.lk[:], T.kk[:], ["kk"], ["lk"])
    cpv(T.lu[:], T.lui[:], ["lui"], ["lu"])
    ts(T.pp[:, 0:32], T.dd[:], 0, 1.0 / UP / L, A.is_equal, A.mult, ["dd"], ["p0"])
    ts(T.pp[:, 32:64], T.dd[:], 1, UP, A.is_equal, A.mult, ["dd"], ["p1"])
    ts(T.pp[:, 64:96], T.dd[:], 2, None, A.is_ge, None, ["dd"], ["p2"])
    ts(T.sm[:, 2:3], T.dd[:, 16:17], 2, UP, A.is_equal, A.mult, ["dd"], ["m1"])
    ts(T.sm[:, 3:4], T.dd[:, 16:17], 1, None, A.is_ge, None, ["dd"], ["m2"])
    ts(T.sm[:, 0:1], T.kk[:, 0:1], 15, None, A.is_equal, None, ["kk"], ["c1"])
    ts(T.sm[:, 1:2], T.kk[:, 0:1], 15, 1.0 / UP, A.is_lt, A.mult, ["kk"], ["c2"])
    ts(T.k20[:], T.kk[:], 20, None, A.mult, None, ["kk"], ["k20"])
    tt(T.pp[:, 96:128], T.pp[:, 32:64], T.pp[:, 64:96], A.add, ["p1", "p2"], ["p12"])
    tt(T.sm[:, 4:5], T.sm[:, 2:3], T.sm[:, 3:4], A.max, ["m1", "m2"], ["m3"])
    tt(T.sm[:, 5:6], T.sm[:, 0:1], T.sm[:, 1:2], A.add, ["c1", "c2"], ["cp"])
    tt(T.pp[:, 128:160], T.pp[:, 96:128], T.pp[:, 0:32], A.add, ["p12", "p0"], ["pm"])
    tt(T.cc[:], T.k20[:], T.ic[:], A.add, ["k20", "ic"], ["cc"])
    tt(T.ee[:], T.e16[:], T.kk[:], A.add, ["e16", "kk"], ["ee"])
    cpv(T.M[:, 0:16], T.pp[:, 128:144], ["pm"], ["Ma"])
    cpv(T.lc[:, 1:21], T.cc[:], ["cc"], ["lc1"])
    cpv(T.lc[:, 0:1], T.k20[:, 0:1], ["k20"], ["lc0"])
    ts(T.qq[:], T.ee[:], -9.5, 0.05, A.add, A.mult, ["ee"], ["qq"])
    ts(T.rr[:, 0:20], T.ee[:], -16.0, 304.0, A.mult, A.add, ["ee"], ["r1"])
    ts(T.rr[:, 20:40], T.qq[:], 321.0, None, A.mult, None, ["qq"], ["r2"])
    tt(T.rr[:, 40:60], T.rr[:, 0:20], T.rr[:, 20:40], A.add, ["r1", "r2"], ["r3"])
    cpv(T.rho[:], T.rr[:, 40:60], ["r3"], ["rho"])
    CP = T.sm[:, 5:6]
    for b in range(4):
        cpa(T.et[:, 512 * b + b:512 * b + 512:4], T.dg[:], ["dg", "etz", "ety"], ["et%d" % b])
    cpa(T.M[:, 16:336], T.pp[:, 144:160].indirect(T.lk[:]), ["pm", "lk"], ["Mb"])
    cpv(T.ls[:], T.sti[:], ["sti"], ["ls"])
    cpa(T.NR[:], T.idn[:].indirect(T.ls[:]), ["idn", "ls"], ["NRa", "NRb"])
    cpa(T.G1[:, :], T.NR[:].indirect(T.lc[:, 0:21]), ["NRa", "NRb", "lc0", "lc1"], ["G1a", "G1b"])
    quant(T.eq[:], T.es[:], T.et[:], ["et0", "et1", "et2", "et3", "etz", "ety"], ["eq"])
    tt(T.M[:, 16:17], T.sm[:, 4:5], T.pp[:, 16:17], A.max, ["m3", "p0"], ["Mb"])

    quant(T.uq[:], T.us[:], T.ui[:], ["ui"], ["uq"])
    cpv(T.urq[:, 0:128].bitcast(dt.uint32), T.uq[:, 0:128].bitcast(dt.uint32).indirect(T.lu[:, 0:8]), ["uq", "lu"], ["urq"])
    cpa(T.urs[:, 0:128], T.us[:, 0:128].indirect(T.lu[:, 0:8]), ["uq", "lu"], ["urs"])
    cpv(T.la[:], T.tai[:], ["tai"], ["la"])
    cpv(T.lb[:], T.tbi[:], ["tbi"], ["lb"])

    def scores(r):
        mm(4, T.urq[:], T.urs[:], T["xq%d" % r][:], T["xs%d" % r][:], ["urq", "urs", "xq%d" % r])

    def unpack(b, q, p):
        mm(b, T.eq[:, 128 * b:128 * b + 128], T.es[:, 128 * b:128 * b + 128], T[q][:], T[p][:], ["eq", q])

    def row(G, E):
        scan(T[E][:, :], T.M[:, :], T[G][:, :], 0.0, A.mult, A.add, [G + "a", G + "b", "Ma", "Mb"], [E])

    def offsets(E, o, less):
        ts(T[o][:, 1:21], T[E][:, 31:336:16], CP, -float(less), A.mult, A.add, [E, "cp"], [o + "m"])
        ts(T[o][:, 0:1], T[E][:, 335:336], CP, -float(less), A.mult, A.add, [E, "cp"], [o + "d"])

    def partner(r):
        other = T.cores[rank ^ STEP[r]]
        return topo.addr(other)[0:2] + (topo.mask(core, other), len(topo.engines(core, other)))

    def send_state(r):
        rid, pid, mask, ne = partner(r)
        xq, xs, rq, rp, sem = [n + str(r) for n in ("xq", "xs", "rq", "rp", "gotz")]
        learn("g", wrote[xq])
        g.remote_dma(T[rq][:, :].bitcast(dt.uint8), T[xq][:, :].bitcast(dt.uint8), T.sem[sem], T.sem.sent, pid, rid, mask)
        g.remote_dma(T[rp][:, :], T[xs][:, :], T.sem[sem], T.sem.sent, pid, rid, mask)
        count["sent"] = count.get("sent", 0) + 2 * ne
        wrote[rq] = [(sem, 2 * ne)]

    quant(T.xq0[:], T.xs0[:], T.xi[:], ["xi"], ["xq0"])
    scores(0)
    for b in range(4):
        unpack(b, "xq0", "xs0")
    row("G1", "E1")
    offsets("E1", "sc", 1)
    send_state(0)
    cpa(T.W6[:, 3:961:3], T.idn[:].indirect(T.la[:]), ["idn", "la"], ["W60"])
    cpa(T.W6[:, 4:962:3], T.idn[:].indirect(T.lb[:]), ["idn", "lb"], ["W61"])
    W6K = ["W60", "W61", "W62", "W6x", "W6y", "W63", "W64", "W65"]
    WK = ["W0", "W1", "W2", "W3", "W4a1", "W4b1", "W5", "Wx", "Wy"]
    less = BIG + BIG // L
    ts(T.tt[:], T.ps4[:, 0:C], 0.0, float(L), A.is_gt, A.mult, ["ps4"], ["tt"])
    plus(T.pk[:], T.tt[:], T.b0[:], ["tt", "b0"], ["pk"])

    for r in range(3):
        rid, pid, mask, ne = partner(r)
        rq, rp, sn, pl, xn = [n + str(r) for n in ("rq", "rp", "sn", "pl", "xn")]
        cpa(T.W[:, 3:961:3], T.pk[:].indirect(T.la[:]), ["pk", "la"], ["W0"])
        cpv(T.G0[:, :], T.pk[:].indirect(T.sc[:, 0:21]), ["pk", "scm", "scd"], ["G0a", "G0b"])
        cpv(T.W[:, 4:962:3], T.pk[:].indirect(T.lb[:]), ["pk", "lb"], ["W1"])
        cpa(T.W[:, 5:963:3], T.W[:, 3:961:3], ["W0"], ["W2"])
        cpg(T.W[:, 2051:3009:3], T.W[:, 3:961:3], ["W0"], ["W3"])
        cpa(T.W[:, 2053:3011:3], T.W[:, 3:961:3], ["W0"], ["W5"])
        row("G0", "E0")
        cpv(T.W[:, 2052:2530:3], T.W[:, 4:482:3], ["W1"], ["W4a1"])
        cpa(T.W[:, 2532:3010:3], T.W[:, 484:962:3], ["W1"], ["W4b1"])
        offsets("E0", "o0", less)
        if r == 0:
            unnamed("W6")
            cpg(T.W6[:, 5:963:3], T.W6[:, 3:961:3], ["W60"], ["W62"])
            cpg(T.W6[:, 2051:3009:3], T.W6[:, 3:961:3], ["W60"], ["W63"])
            cpg(T.W6[:, 2052:3010:3], T.W6[:, 4:962:3], ["W61"], ["W64"])
            cpg(T.W6[:, 2053:3011:3], T.W6[:, 3:961:3], ["W60"], ["W65"])
            iota(T.b4[:], [[1, C]], BIG, 0, "b4", True)
        gaps = [(T["t%d" % b][:], T["ps%d" % b][:, 0:C], ["ps%d" % b], ["t%d" % b], b) for b in range(4)]
        gaps += [(T["w%d" % b][:], T["ps%d" % b][:, 0:C], ["ps%d" % b], ["w%d" % b], None) for b in range(2)]
        for n in range(1, STAGES + 1):
            o, G, E, on = "o%d" % ((n + 1) % 2), "G%d" % (n % 2), "E%d" % (n % 2), "o%d" % (n % 2)
            win, wk = (T.W, WK) if n < STAGES else (T.W6, W6K)
            cpv(T[G][:, 0:16 * CUT], win[:, 0:3011].indirect(T[o][:, 0:CUT]), wk + [o + "m", o + "d"], [G + "a"])
            cpa(T[G][:, 16 * CUT:336], win[:, 0:3011].indirect(T[o][:, CUT:21]), wk + [o + "m"], [G + "b"])
            if n < STAGES:
                for out, in_, rd, wr, b in [gaps.pop(0) for i in range(2 if n == 1 else 1)]:
                    cpa(out, in_, rd, wr)
                    if b is not None:
                        unpack(b, rq, rp)
                row(G, E)
                offsets(E, on, less)
        cpv(T.NR[:, 0:160], T.G0[:, 16:336].indirect(T.rho[:, 0:10]), ["G0a", "G0b", "rho"], ["NRa"])
        cpa(T.NR[:, 160:320], T.G0[:, 16:336].indirect(T.rho[:, 10:20]), ["G0a", "G0b", "rho"], ["NRb"])
        if r == 0:
            cpa(T.M0[:], T.pp[:, 112:128].indirect(T.lk[:]), ["p12", "lk"], ["M0"])
        scan(T.EN[:], T.M[:, 16:336], T.NR[:], 0.0, A.mult, A.add, ["NRa", "NRb", "Mb"], ["EN"])
        ts(T[sn][:], T.EN[:, 15:320:16], CP, -1.0, A.mult, A.add, ["EN", "cp"], [sn])
        learn("g", wrote[sn])
        g.remote_dma(T[pl][:, :], T[sn][:, :], T.sem["gotl%d" % r], T.sem.sent, pid, rid, mask)
        count["sent"] += ne
        wrote[pl] = [("gotl%d" % r, ne)]
        for b in range(4):
            (cpv if b < 2 else cpa)(T.z[:, b:4 * C:4], T["t%d" % b][:].indirect(T[sn][:]), ["t%d" % b, sn], ["z%d" % b])
        for b in range(2, 4):
            (cpv if b == 2 else cpa)(T["w%d" % b][:], T["ps%d" % b][:, 0:C], ["ps%d" % b], ["w%d" % b])
        for b in range(4):
            (cpv if b < 2 else cpa)(T.za[:, b:4 * C:4], T["w%d" % b][:].indirect(T[pl][:]), ["w%d" % b, pl], ["za%d" % b])
        quant(T.zq[:], T.zp[:], T.za[:], ["za%d" % b for b in range(4)], ["zq"])
        for b in range(4):
            mm(b, T.wq[:, 128 * b:128 * b + 128], T.wp[:, 128 * b:128 * b + 128], T.zq[:], T.zp[:], ["wq", "wp", "zq"])
        if r < 2:
            row("G0", "E1")
            offsets("E1", "sc", 1)
        if r == 0:
            quant(T.vq[:], T.vs[:], T.vi[:], ["vi"], ["vq"])
        if r == 2:
            ts(T.x320[:], T.x12[:], 320.0, None, A.mult, None, ["x12"], ["x320"])
            plus(T.b4s[:], T.x320[:], T.b4[:], ["x320", "b4"], ["b4s"])
            op("a", lambda: S.activation(T.ob[:, 0:320], T.NR[:], ACT.Identity, bias=-1.0), ["NRa", "NRb"], ["obs"])
            store("ops", T.op[:, 0:320], T.ob[0:128:16, 0:320], ["obs"])
        for b in range(4):
            hb, pb = T["h%d" % b], T["ps%d" % b]
            op("a", lambda: S.activation(hb[:], pb[:, 0:C], ACT.Copy, scale=0.03125), ["ps%d" % b], ["h%d" % b])
            tt(T[xn][:, b:4 * C:4], hb[:].indirect(T[pl][:]), T.z[:, b:4 * C:4], A.add, ["h%d" % b, pl, "z%d" % b], [xn + str(b)])
        for b in range(4):
            cpa(T.ht[:, b:4 * C:4], T["h%d" % b][:], ["h%d" % b], ["ht%d" % b])
        if r == 1:
            for i, key in enumerate(("W4a", "W4b", "W4c", "W4d")):
                cpg(T.W4[:, 320 * i:320 * i + 320], T.W6[:, 3 + i % 2:961 + i % 2:3], ["W6%d" % (i % 2)], [key])
        xq, xs = "xq%d" % (r + 1), "xs%d" % (r + 1)
        if r < 2:
            quant(T[xq][:], T[xs][:], T[xn][:], [xn + str(b) for b in range(4)], [xq])
            scores(r + 1)
            send_state(r + 1)
            quant(T.hq[:], T.hp[:], T.ht[:], ["ht%d" % b for b in range(4)], ["hq"])
            mm(5, T.urq[:], T.urs[:], T.hq[:], T.hp[:], ["urq", "urs", "hq"])
            for b in range(4):
                unpack(b, xq, xs)
            gk = "g%d" % (r + 1)
            ts(T.tt[:], T.ps4[:, 0:C], 0.0, float(L), A.is_gt, A.mult, ["ps4"], ["tt"])
            ts(T[gk][:], T.ps5[:, 0:C], 0.0, None, A.is_gt, None, ["ps5"], [gk])
            plus(T.uu[:], T.tt[:], T.b0[:], ["tt", "b0"], ["uu"])
            if r == 1:
                tt(T.x12[:], T.g1[:], T.g2[:], A.not_equal, ["g1", "g2"], ["x12"])
                gk = "x12"
            plus(T.pk[:], T[gk][:], T.uu[:], [gk, "uu"], ["pk"])
    quant(T.hq[:], T.hp[:], T.ht[:], ["ht%d" % b for b in range(4)], ["hq"])
    mm(5, T.urq[:], T.urs[:], T.hq[:], T.hp[:], ["urq", "urs", "hq"])
    quant(T.xq3[:], T.xs3[:], T.xn2[:], ["xn2%d" % b for b in range(4)], ["xq3"])
    mm(6, T.vq[:], T.vs[:], T.xq3[:], T.xs3[:], ["vq", "xq3"])
    store("oc", T.oc[:, :], T.xq3[:, :].bitcast(dt.uint8), ["xq3"])
    for k in range(4):
        store("os%d" % k, T.osc[4 * k:4 * k + 4, :], T.xs3[32 * k:32 * k + 4, :], ["xq3"])
    cpa(T.yb[:], T.ps6[:, 0:C], ["ps6"], ["yb"])
    store("y", T.y[:, :], T.yb[:], ["yb"])
    ts(T.g3[:], T.ps5[:, 0:C], 0.0, 320.0, A.is_gt, A.mult, ["ps5"], ["g3"])
    plus(T.fin[:], T.g3[:], T.b4s[:], ["g3", "b4s"], ["fin"])
    scan(T.EN[:], T.M0[:], T.fin[:], 0.0, A.mult, A.add, ["fin", "M0"], ["EN"])
    ts(T.lfa[:], T.EN[:, 15:320:16], CP, -float(BIG), A.mult, A.add, ["EN", "cp"], ["lfa"])
    ts(T.lfb[:], T.EN[:, 15:320:16], CP, 320.0 - BIG, A.mult, A.add, ["EN", "cp"], ["lfb"])
    w4 = ["W4a", "W4b", "W4c", "W4d"]
    op("a", lambda: S.activation(T.ob[:, 320:640], T.W4[:, :].indirect(T.lfa[:]), ACT.Identity, bias=-1.0), w4 + ["lfa"], ["oba"])
    ts(T.ob[:, 640:960], T.W4[:, :].indirect(T.lfb[:]), -1.0, None, A.add, None, w4 + ["lfb"], ["obb"])
    store("opt", T.op[:, 320:960], T.ob[0:128:16, 320:960], ["oba", "obb"])
    learn("g", [(s, n) for s, n in count.items()])
